import numpy as np
import ml_dtypes


def mxq(x, axis, fmt="e4m3"):
    dtype, down = {"e4m3": (ml_dtypes.float8_e4m3fn, 7), "e5m2": (ml_dtypes.float8_e5m2, 14)}[fmt]
    v = np.moveaxis(np.asarray(x, np.float32).astype(ml_dtypes.bfloat16).astype(np.float64), axis, -1)
    blocks = v.reshape(v.shape[:-1] + (-1, 32))
    amax = np.abs(blocks).max(-1, keepdims=True)
    byte = np.maximum(np.where(amax > 0, np.frexp(amax)[1] - 1 + 127, 0) - down, 1)
    scale = np.exp2(byte - 127.0)
    codes = (blocks / scale).astype(np.float32).astype(dtype).astype(np.float64)
    return np.moveaxis((codes * scale).reshape(v.shape), -1, axis)


WIDE = False


def mx_kscale(k):
    if not WIDE:
        return np.ones(k)
    levels = np.array([10, -10, 5, -5, 0])
    if k % 512:
        return np.exp2(np.random.permutation(np.resize(levels, k // 32))).repeat(32)
    a = np.empty((k // 512, 16))
    for p in range(k // 512):
        a[p, :8] = np.random.permutation(np.resize(levels, 8))
        for g in range(8):
            far = levels[np.abs(levels - a[p, g]) >= 10]
            a[p, g + 8] = far[np.random.randint(len(far))]
    return np.exp2(a.ravel()).repeat(32)


def f64(x):
    return np.asarray(x).astype(np.float64)


def striped(idx):
    return np.tile(np.asarray(idx).reshape(-1, 16).T, (8, 1)).astype(np.uint16)


def unstriped(offs):
    return offs[:16].T.reshape(-1).astype(np.int64)


def striped8(idx):
    return np.asarray(idx).reshape(8, -1, 16).transpose(0, 2, 1).reshape(128, -1).astype(np.uint16)


def unstriped8(offs):
    return offs.reshape(8, 16, -1).transpose(0, 2, 1).reshape(8, -1).astype(np.int64)


def pick8(x, idx, run):
    r = np.arange(len(x))
    return x[r[:, None], idx[r % (8 * run) // run]]


E2M1 = np.array([0.0, 0.5, 1.0, 1.5, 2.0, 3.0, 4.0, 6.0, -0.0, -0.5, -1.0, -1.5, -2.0, -3.0, -4.0, -6.0])


def pack_weight(w, fmt):
    k, n = w.shape
    w = f64(np.asarray(w, np.float32).astype(ml_dtypes.bfloat16)).reshape(k // 32, 32, n)
    amax = np.abs(w).max(1)
    if fmt == "e4m3":
        byte = np.frexp(amax)[1] - 1 + 127 - 7
    else:
        mant, ex = np.frexp(amax / 6.0)
        byte = np.where(mant > 0.5, ex, ex - 1) + 127
    byte = np.clip(np.where(amax > 0, byte, 1), 1, 254)
    scaled = (w * np.exp2(127.0 - byte)[:, None, :]).reshape(k, n).astype(np.float32)
    by_word = np.ascontiguousarray(scaled.reshape(k // 512, 128, 4, n).transpose(0, 1, 3, 2))
    if fmt == "e4m3":
        words = by_word.astype(ml_dtypes.float8_e4m3fn).view(np.uint8)
    else:
        c = by_word.astype(ml_dtypes.float4_e2m1fn).view(np.uint8) & 0xF
        words = (c[..., 0::2] | (c[..., 1::2] << 4)).reshape(k // 512, 128, 2 * n)
    return np.ascontiguousarray(words), np.ascontiguousarray(byte.astype(np.uint8).reshape(k // 512, 16, n))


def unpack_weight(words, scales, fmt):
    g, _, n = scales.shape
    words = np.ascontiguousarray(words).reshape(g, 128, n, -1)
    if fmt == "e4m3":
        vals = words.view(ml_dtypes.float8_e4m3fn).astype(np.float64)
    else:
        nib = np.empty((g, 128, n, 4), np.uint8)
        nib[..., 0::2] = words & 0xF
        nib[..., 1::2] = words >> 4
        vals = E2M1[nib]
    vals = vals * np.repeat(np.exp2(scales.astype(np.float64) - 127.0), 8, axis=1)[..., None]
    return vals.transpose(0, 1, 3, 2).reshape(g * 512, n)


K, J, R, T, Z, M, O, C, N, S = 512, 512, 512, 1024, 512, 1024, 256, 512, 256, 1024


def setup_inputs():
    n = np.random.standard_normal
    idx = np.random.permutation(T)[:J]
    idx2 = np.random.permutation(M)[:J]
    idx3 = np.stack([np.random.permutation(J)[:O] for _ in range(8)])
    idx4 = np.stack([np.random.permutation(J)[:O] for _ in range(8)])
    idx5 = np.stack([np.random.permutation(C)[:O] for _ in range(8)])
    idx6 = np.stack([np.random.permutation(C)[:O] for _ in range(8)])
    idx7 = np.random.permutation(S)[:N]
    fk = mx_kscale(K)
    fr = mx_kscale(R)
    fz = mx_kscale(Z)
    xtp = pack_weight(n((K, T)) * fk[:, None], "e4m3")
    wp = pack_weight(n((K, R)) * 1 / np.sqrt(K) / fk[:, None] * fr, "e2m1")
    xop = pack_weight(n((Z, M)) / fz[:, None], "e2m1")
    w2p = pack_weight(n((Z, R)) * 1 / np.sqrt(Z) * fz[:, None] * fr, "e4m3")
    vsp = pack_weight(n((R, S)) * 1 / np.sqrt(R) / fr[:, None], "e4m3")
    return {
        "xt_words": xtp[0],
        "xt_scales": xtp[1],
        "w_words": wp[0],
        "w_scales": wp[1],
        "xo_words": xop[0],
        "xo_scales": xop[1],
        "w2_words": w2p[0],
        "w2_scales": w2p[1],
        "sa": (np.random.uniform(0.5, 1.6, (R, 1))).astype(np.float32),
        "sb": (np.random.uniform(0.5, 1.6, (R, 1))).astype(np.float32),
        "vs_words": vsp[0],
        "vs_scales": vsp[1],
        "offs": striped(idx),
        "offs2": striped(idx2),
        "offs3": striped8(idx3),
        "offs4": striped8(idx4),
        "offs5": striped8(idx5),
        "offs6": striped8(idx6),
        "offs7": striped(idx7),
    }


def reference(xt_words, xt_scales, w_words, w_scales, xo_words, xo_scales, w2_words, w2_scales, sa, sb, vs_words, vs_scales, offs, offs2, offs3, offs4, offs5, offs6, offs7):
    idx = unstriped(offs)
    idx2 = unstriped(offs2)
    idx3 = unstriped8(offs3)
    idx4 = unstriped8(offs4)
    idx5 = unstriped8(offs5)
    idx6 = unstriped8(offs6)
    idx7 = unstriped(offs7)
    xtu = unpack_weight(xt_words, xt_scales, "e4m3")
    wu = unpack_weight(w_words, w_scales, "e2m1")
    xou = unpack_weight(xo_words, xo_scales, "e2m1")
    w2u = unpack_weight(w2_words, w2_scales, "e4m3")
    vsu = unpack_weight(vs_words, vs_scales, "e4m3")
    xtidxg = xtu[:, idx]
    xoidx2g = xou[:, idx2]
    a = wu.T @ xtidxg + w2u.T @ xoidx2g
    f1 = pick8(a, idx3, 64) * f64(sa)
    f2 = pick8(a, idx4, 64) * f64(sb)
    lo = np.minimum(f1, f2)
    hi = np.maximum(f1, f2)
    pl = np.zeros((R, C))
    pl[np.arange(R)[:, None], idx5[np.arange(R) % 512 // 64]] = lo
    pu = np.zeros((R, C))
    pu[np.arange(R)[:, None], idx6[np.arange(R) % 512 // 64]] = hi
    hid = pl + pu
    vsidx7g = vsu[:, idx7]
    hidq = mxq(hid, 0, "e4m3")
    y = vsidx7g.T @ hidq
    return y

@@ -1,0 +1,194 @@
+from contextlib import ExitStack
+
+import concourse.mybir as mybir
+
+K, J, R, T, Z, M, O, C, N, S = 512, 512, 512, 1024, 512, 1024, 256, 512, 256, 1024
+FLOPS = 2 * K * R * J + 2 * Z * R * J + 2 * R * N * C
+
+F32 = mybir.dt.float32
+BF16 = mybir.dt.bfloat16
+I32 = mybir.dt.int32
+U32 = mybir.dt.uint32
+U16 = mybir.dt.uint16
+U8 = mybir.dt.uint8
+FP8X4 = mybir.dt.float8_e4m3fn_x4
+FP4X4 = mybir.dt.float4_e2m1fn_x4
+COPY = mybir.ActivationFunctionType.Copy
+ALU = mybir.AluOpType
+
+P = 128
+PACK = 4
+QUADRANTS = 4
+HALF = 256
+
+
+def tile_picked_tokens_plain_bank_compareexchange_store_plain_kernel(
+    tc, xt_words, xt_scales, w_words, w_scales, xo_words, xo_scales, w2_words, w2_scales,
+    sa, sb, vs_words, vs_scales, offs, offs2, offs3, offs4, offs5, offs6, offs7, out,
+):
+    nc = tc.nc
+    with ExitStack() as ctx:
+        lists = ctx.enter_context(tc.tile_pool(name="lists", bufs=1))
+        pool = ctx.enter_context(tc.tile_pool(name="pool", bufs=1))
+        psum = ctx.enter_context(tc.psum_pool(name="psum", bufs=1))
+
+        def sbuf(name, cols, dtype):
+            return pool.tile([P, cols], dtype, name=name, align_bytes=64)
+
+        def load_list(name, source):
+            tile = lists.tile(list(source.shape), U16, name=name)
+            nc.sync.dma_start(tile[:], source)
+            return tile
+
+        def load_e4m3_words(queue, name, source, cols):
+            tile = sbuf(name, cols, U32)
+            queue.dma_start(tile[:].bitcast(I32), source[0].rearrange("p n t -> p (n t)").bitcast(I32))
+            return tile
+
+        def load_e2m1_words(queue, name, source, cols):
+            tile = sbuf(name, cols, U16)
+            queue.dma_start(tile[:].bitcast(I32), source[0].bitcast(I32))
+            return tile
+
+        def load_scales(queues, name, source, cols):
+            tile = sbuf(name, cols, U8)
+            for q in range(QUADRANTS):
+                rows = source[0, 4 * q : 4 * q + 4, :].bitcast(I32)
+                queues[q].dma_start(tile[32 * q : 32 * q + 32, :].bitcast(I32), rows.partition_broadcast(8))
+            return tile
+
+        def load_row_factors(name, source):
+            tile = pool.tile([P, PACK], F32, name=name)
+            nc.sync.dma_start(tile[:], source.rearrange("(p t) o -> p (t o)", t=PACK))
+            return tile
+
+        sync4 = [nc.sync] * QUADRANTS
+        list2 = load_list("list2", offs2)
+        xo_s = load_scales([nc.sync, nc.scalar, nc.sync, nc.scalar], "xo_s", xo_scales, M)
+        xo_w = load_e2m1_words(nc.scalar, "xo_w", xo_words, M)
+        list1 = load_list("list1", offs)
+        xt_w = load_e4m3_words(nc.scalar, "xt_w", xt_words, T)
+        w2_s = load_scales(sync4, "w2_s", w2_scales, R)
+        w2_w = load_e4m3_words(nc.sync, "w2_w", w2_words, R)
+        xt_s = load_scales(sync4, "xt_s", xt_scales, T)
+        w_s = load_scales(sync4, "w_s", w_scales, R)
+        w_w = load_e2m1_words(nc.sync, "w_w", w_words, R)
+        list3 = load_list("list3", offs3)
+        sa_t = load_row_factors("sa_t", sa)
+        list4 = load_list("list4", offs4)
+        sb_t = load_row_factors("sb_t", sb)
+        list5 = load_list("list5", offs5)
+        list6 = load_list("list6", offs6)
+        list7 = load_list("list7", offs7)
+        vs_w = load_e4m3_words(nc.sync, "vs_w", vs_words, S)
+        vs_s = load_scales(sync4, "vs_s", vs_scales, S)
+
+        pl = [sbuf("pl%d" % i, C, F32) for i in range(2)]
+        pu = [sbuf("pu%d" % i, C, F32) for i in range(2)]
+        for page in pl + pu:
+            nc.vector.memset(page[:], 0.0)
+
+        xo_sg = sbuf("xo_sg", J, U8)
+        xo_wg = sbuf("xo_wg", J, U16)
+        xt_wg = sbuf("xt_wg", J, U32)
+        xt_sg = sbuf("xt_sg", J, U8)
+        nc.vector.tensor_copy(xo_sg[:], xo_s[:].indirect(list2[:]))
+        nc.vector.tensor_copy(xo_wg[:], xo_w[:].indirect(list2[:]))
+        nc.vector.tensor_copy(xt_wg[:], xt_w[:].indirect(list1[:]))
+
+        w2_wd = sbuf("w2_wd", R, U32)
+        w2_sd = sbuf("w2_sd", R, U8)
+        w_wd = sbuf("w_wd", R, U16)
+        w_sd = sbuf("w_sd", R, U8)
+        for dealt, raw in ((w2_wd, w2_w), (w_wd, w_w)):
+            nc.scalar.copy(dealt[:].rearrange("p (t m) -> p m t", t=PACK), raw[:].rearrange("p (m t) -> p m t", t=PACK))
+        for dealt, raw in ((w2_sd, w2_s), (w_sd, w_s)):
+            nc.gpsimd.tensor_copy(dealt[:].rearrange("p (t m) -> p t m", t=PACK), raw[:].rearrange("p (m t) -> p t m", t=PACK))
+
+        pieces = [(0, slice(0, HALF)), (0, slice(HALF, J))] + [(t, slice(0, J)) for t in range(1, PACK)]
+        acc = [psum.tile([P, cols.stop - cols.start], F32, name="acc%d" % i) for i, (t, cols) in enumerate(pieces)]
+        a = [sbuf("a%d" % t, J, F32) for t in range(PACK)]
+
+        for i, (t, cols) in enumerate(pieces):
+            rows = slice(P * t, P * (t + 1))
+            nc.tensor.matmul_mx(
+                acc[i][:], lhsT=w2_wd[:, rows].bitcast(FP8X4), lhsT_scale=w2_sd[:, rows],
+                rhs=xo_wg[:, cols].bitcast(FP4X4), rhs_scale=xo_sg[:, cols], start=True, stop=False,
+            )
+
+        def close_piece(i):
+            t, cols = pieces[i]
+            rows = slice(P * t, P * (t + 1))
+            nc.tensor.matmul_mx(
+                acc[i][:], lhsT=w_wd[:, rows].bitcast(FP4X4), lhsT_scale=w_sd[:, rows],
+                rhs=xt_wg[:, cols].bitcast(FP8X4), rhs_scale=xt_sg[:, cols], start=False, stop=True,
+            )
+            if t == 0:
+                nc.scalar.copy(a[t][:, cols], acc[i][:])
+            else:
+                nc.vector.tensor_copy(a[t][:, cols], acc[i][:])
+
+        for h in range(2):
+            nc.vector.tensor_copy(
+                xt_sg[:, HALF * h : HALF * (h + 1)], xt_s[:].indirect(list1[:, 16 * h : 16 * (h + 1)])
+            )
+            close_piece(h)
+        for i in range(2, len(pieces)):
+            close_piece(i)
+
+        lo = [sbuf("lo%d" % t, O, F32) for t in range(PACK)]
+        hi = [sbuf("hi%d" % t, O, F32) for t in range(PACK)]
+        hid4 = [sbuf("hid4_%d" % h, PACK * HALF, BF16) for h in range(2)]
+
+        def compare(t):
+            f1 = sbuf("f1_%d" % t, O, F32)
+            f2 = sbuf("f2_%d" % t, O, F32)
+            nc.scalar.activation(f1[:], a[t][:].indirect(list3[:]), COPY, scale=sa_t[:, t : t + 1])
+            nc.scalar.activation(f2[:], a[t][:].indirect(list4[:]), COPY, scale=sb_t[:, t : t + 1])
+            nc.vector.tensor_tensor(lo[t][:], f1[:], f2[:], ALU.min)
+            nc.vector.tensor_tensor(hi[t][:], f1[:], f2[:], ALU.max)
+
+        def place(t):
+            nc.scalar.activation(pl[t % 2][:].indirect(list5[:]), lo[t][:], COPY)
+            nc.scalar.activation(pu[t % 2][:].indirect(list6[:]), hi[t][:], COPY)
+
+        def add_up(t):
+            hid = [sbuf("hid%d_%d" % (t, h), HALF, BF16) for h in range(2)]
+            for h in range(2):
+                cols = slice(HALF * h, HALF * (h + 1))
+                nc.vector.tensor_tensor(hid[h][:], pl[t % 2][:, cols], pu[t % 2][:, cols], ALU.add)
+            for h in range(2):
+                nc.vector.tensor_copy(hid4[h][:, t : PACK * HALF : PACK], hid[h][:])
+
+        vs_wg = sbuf("vs_wg", N, U32)
+        vs_sg = sbuf("vs_sg", N, U8)
+        compare(0)
+        for t in range(PACK):
+            if t + 1 < PACK:
+                compare(t + 1)
+            place(t)
+            if t == 0:
+                nc.vector.tensor_copy(vs_wg[:], vs_w[:].indirect(list7[:]))
+                nc.vector.tensor_copy(vs_sg[:], vs_s[:].indirect(list7[:]))
+            add_up(t)
+
+        codes = [sbuf("codes%d" % h, HALF, U32) for h in range(2)]
+        scales = [sbuf("scales%d" % h, HALF, U8) for h in range(2)]
+        for h in range(2):
+            nc.vector.quantize_mx(out=codes[h][:].bitcast(FP8X4), scales=scales[h][:], in_=hid4[h][:])
+        for h in range(2):
+            cols = slice(HALF * h, HALF * (h + 1))
+            for b in range(2):
+                rows = slice(P * b, P * (b + 1))
+                y = psum.tile([P, HALF], F32, name="y%d_%d" % (h, b), tag=("y%d" % b) if h == 0 else ("acc%d" % b))
+                nc.tensor.matmul_mx(
+                    y[:], lhsT=vs_wg[:, rows].bitcast(FP8X4), lhsT_scale=vs_sg[:, rows],
+                    rhs=codes[h][:].bitcast(FP8X4), rhs_scale=scales[h][:], start=True, stop=True,
+                )
+                result = sbuf("result%d_%d" % (h, b), HALF, F32)
+                if h == 1 and b == 1:
+                    nc.vector.tensor_copy(result[:], y[:])
+                    nc.sync.dma_start(out[rows, cols], result[:])
+                else:
+                    nc.scalar.copy(result[:], y[:])
+                    (nc.scalar if h == 1 else nc.sync).dma_start(out[rows, cols], result[:])

@@ -50,11 +50,14 @@ def tile_picked_tokens_plain_bank_compareexchange_store_plain_kernel(
             queue.dma_start(tile[:].bitcast(I32), source[0].bitcast(I32))
             return tile
 
-        def load_scales(queues, name, source, cols):
-            tile = sbuf(name, cols, U8)
-            for q in range(QUADRANTS):
+        def load_scale_rows(queues, tile, source, quadrants):
+            for q in quadrants:
                 rows = source[0, 4 * q : 4 * q + 4, :].bitcast(I32)
                 queues[q].dma_start(tile[32 * q : 32 * q + 32, :].bitcast(I32), rows.partition_broadcast(8))
+
+        def load_scales(queues, name, source, cols):
+            tile = sbuf(name, cols, U8)
+            load_scale_rows(queues, tile, source, range(QUADRANTS))
             return tile
 
         def load_row_factors(name, source):
@@ -64,15 +67,17 @@ def tile_picked_tokens_plain_bank_compareexchange_store_plain_kernel(
 
         sync4 = [nc.sync] * QUADRANTS
         list2 = load_list("list2", offs2)
-        xo_s = load_scales([nc.sync, nc.scalar, nc.sync, nc.scalar], "xo_s", xo_scales, M)
         xo_w = load_e2m1_words(nc.scalar, "xo_w", xo_words, M)
+        xo_s = load_scales([nc.sync, nc.scalar, nc.sync, nc.scalar], "xo_s", xo_scales, M)
         list1 = load_list("list1", offs)
         xt_w = load_e4m3_words(nc.scalar, "xt_w", xt_words, T)
         w2_s = load_scales(sync4, "w2_s", w2_scales, R)
+        xt_s = sbuf("xt_s", T, U8)
+        load_scale_rows(sync4, xt_s, xt_scales, range(0, 2))
         w2_w = load_e4m3_words(nc.sync, "w2_w", w2_words, R)
-        xt_s = load_scales(sync4, "xt_s", xt_scales, T)
-        w_s = load_scales(sync4, "w_s", w_scales, R)
         w_w = load_e2m1_words(nc.sync, "w_w", w_words, R)
+        load_scale_rows(sync4, xt_s, xt_scales, range(2, QUADRANTS))
+        w_s = load_scales(sync4, "w_s", w_scales, R)
         list3 = load_list("list3", offs3)
         sa_t = load_row_factors("sa_t", sa)
         list4 = load_list("list4", offs4)
@@ -85,56 +90,69 @@ def tile_picked_tokens_plain_bank_compareexchange_store_plain_kernel(
 
         pl = [sbuf("pl%d" % i, C, F32) for i in range(2)]
         pu = [sbuf("pu%d" % i, C, F32) for i in range(2)]
-        for page in pl + pu:
-            nc.vector.memset(page[:], 0.0)
+        for engine, i in ((nc.vector, 0), (nc.gpsimd, 1)):
+            engine.memset(pl[i][:], 0.0)
+            engine.memset(pu[i][:], 0.0)
 
         xo_sg = sbuf("xo_sg", J, U8)
         xo_wg = sbuf("xo_wg", J, U16)
         xt_wg = sbuf("xt_wg", J, U32)
         xt_sg = sbuf("xt_sg", J, U8)
-        nc.vector.tensor_copy(xo_sg[:], xo_s[:].indirect(list2[:]))
         nc.vector.tensor_copy(xo_wg[:], xo_w[:].indirect(list2[:]))
+        nc.vector.tensor_copy(xo_sg[:], xo_s[:].indirect(list2[:]))
         nc.vector.tensor_copy(xt_wg[:], xt_w[:].indirect(list1[:]))
 
         w2_wd = sbuf("w2_wd", R, U32)
         w2_sd = sbuf("w2_sd", R, U8)
         w_wd = sbuf("w_wd", R, U16)
         w_sd = sbuf("w_sd", R, U8)
+        early, late = slice(0, 2), slice(2, PACK)
         for dealt, raw in ((w2_wd, w2_w), (w_wd, w_w)):
-            nc.scalar.copy(dealt[:].rearrange("p (t m) -> p m t", t=PACK), raw[:].rearrange("p (m t) -> p m t", t=PACK))
-        for dealt, raw in ((w2_sd, w2_s), (w_sd, w_s)):
-            nc.gpsimd.tensor_copy(dealt[:].rearrange("p (t m) -> p t m", t=PACK), raw[:].rearrange("p (m t) -> p t m", t=PACK))
+            for tiles in (early, late):
+                nc.scalar.copy(
+                    dealt[:].rearrange("p (t m) -> p m t", t=PACK)[:, :, tiles],
+                    raw[:].rearrange("p (m t) -> p m t", t=PACK)[:, :, tiles],
+                )
+        for dealt, raw, tiles in ((w2_sd, w2_s, slice(0, PACK)), (w_sd, w_s, early), (w_sd, w_s, late)):
+            nc.gpsimd.tensor_copy(
+                dealt[:].rearrange("p (t m) -> p t m", t=PACK)[:, tiles, :],
+                raw[:].rearrange("p (m t) -> p t m", t=PACK)[:, tiles, :],
+            )
 
         pieces = [(0, slice(0, HALF)), (0, slice(HALF, J))] + [(t, slice(0, J)) for t in range(1, PACK)]
         acc = [psum.tile([P, cols.stop - cols.start], F32, name="acc%d" % i) for i, (t, cols) in enumerate(pieces)]
         a = [sbuf("a%d" % t, J, F32) for t in range(PACK)]
 
-        for i, (t, cols) in enumerate(pieces):
+        def notes_pass(i, first):
+            t, cols = pieces[i]
             rows = slice(P * t, P * (t + 1))
             nc.tensor.matmul_mx(
                 acc[i][:], lhsT=w2_wd[:, rows].bitcast(FP8X4), lhsT_scale=w2_sd[:, rows],
-                rhs=xo_wg[:, cols].bitcast(FP4X4), rhs_scale=xo_sg[:, cols], start=True, stop=False,
+                rhs=xo_wg[:, cols].bitcast(FP4X4), rhs_scale=xo_sg[:, cols], start=first, stop=not first,
             )
 
-        def close_piece(i):
+        def tokens_pass(i, first):
             t, cols = pieces[i]
             rows = slice(P * t, P * (t + 1))
             nc.tensor.matmul_mx(
                 acc[i][:], lhsT=w_wd[:, rows].bitcast(FP4X4), lhsT_scale=w_sd[:, rows],
-                rhs=xt_wg[:, cols].bitcast(FP8X4), rhs_scale=xt_sg[:, cols], start=False, stop=True,
+                rhs=xt_wg[:, cols].bitcast(FP8X4), rhs_scale=xt_sg[:, cols], start=first, stop=not first,
             )
-            if t == 0:
-                nc.scalar.copy(a[t][:, cols], acc[i][:])
-            else:
-                nc.vector.tensor_copy(a[t][:, cols], acc[i][:])
 
+        notes_pass(0, True)
+        notes_pass(1, True)
+        notes_pass(2, True)
         for h in range(2):
-            nc.vector.tensor_copy(
-                xt_sg[:, HALF * h : HALF * (h + 1)], xt_s[:].indirect(list1[:, 16 * h : 16 * (h + 1)])
-            )
-            close_piece(h)
-        for i in range(2, len(pieces)):
-            close_piece(i)
+            cols = pieces[h][1]
+            nc.vector.tensor_copy(xt_sg[:, cols], xt_s[:].indirect(list1[:, 16 * h : 16 * (h + 1)]))
+            tokens_pass(h, False)
+            nc.scalar.copy(a[0][:, cols], acc[h][:])
+        tokens_pass(2, False)
+        nc.vector.tensor_copy(a[1][:], acc[2][:])
+        for t in range(2, PACK):
+            tokens_pass(t + 1, True)
+            notes_pass(t + 1, False)
+            nc.vector.tensor_copy(a[t][:], acc[t + 1][:])
 
         lo = [sbuf("lo%d" % t, O, F32) for t in range(PACK)]
         hi = [sbuf("hi%d" % t, O, F32) for t in range(PACK)]

@@ -53,10 +53,15 @@ def tile_picked_tokens_plain_bank_compareexchange_store_plain_kernel(
         def load_scale_rows(queues, tile, source, quadrants):
             for q in quadrants:
                 rows = source[0, 4 * q : 4 * q + 4, :].bitcast(I32)
-                queues[q].dma_start(tile[32 * q : 32 * q + 32, :].bitcast(I32), rows.partition_broadcast(8))
+                queues[q].dma_start(tile[32 * q : 32 * q + 4, :].bitcast(I32), rows)
 
-        def load_scales(queues, name, source, cols):
+        def zeroed_scales(engine, name, cols):
             tile = sbuf(name, cols, U8)
+            engine.memset(tile[:].bitcast(I32), 0)
+            return tile
+
+        def load_scales(queues, name, source, cols, engine=nc.vector):
+            tile = zeroed_scales(engine, name, cols)
             load_scale_rows(queues, tile, source, range(QUADRANTS))
             return tile
 
@@ -68,11 +73,11 @@ def tile_picked_tokens_plain_bank_compareexchange_store_plain_kernel(
         sync4 = [nc.sync] * QUADRANTS
         list2 = load_list("list2", offs2)
         xo_w = load_e2m1_words(nc.scalar, "xo_w", xo_words, M)
-        xo_s = load_scales([nc.sync, nc.scalar, nc.sync, nc.scalar], "xo_s", xo_scales, M)
+        xo_s = load_scales([nc.sync, nc.scalar, nc.sync, nc.scalar], "xo_s", xo_scales, M, nc.gpsimd)
         list1 = load_list("list1", offs)
         xt_w = load_e4m3_words(nc.scalar, "xt_w", xt_words, T)
         w2_s = load_scales(sync4, "w2_s", w2_scales, R)
-        xt_s = sbuf("xt_s", T, U8)
+        xt_s = zeroed_scales(nc.vector, "xt_s", T)
         load_scale_rows(sync4, xt_s, xt_scales, range(0, 2))
         w2_w = load_e4m3_words(nc.sync, "w2_w", w2_words, R)
         w_w = load_e2m1_words(nc.sync, "w_w", w_words, R)
@@ -82,11 +87,11 @@ def tile_picked_tokens_plain_bank_compareexchange_store_plain_kernel(
         sa_t = load_row_factors("sa_t", sa)
         list4 = load_list("list4", offs4)
         sb_t = load_row_factors("sb_t", sb)
-        list5 = load_list("list5", offs5)
-        list6 = load_list("list6", offs6)
         list7 = load_list("list7", offs7)
         vs_w = load_e4m3_words(nc.sync, "vs_w", vs_words, S)
         vs_s = load_scales(sync4, "vs_s", vs_scales, S)
+        list5 = load_list("list5", offs5)
+        list6 = load_list("list6", offs6)
 
         pl = [sbuf("pl%d" % i, C, F32) for i in range(2)]
         pu = [sbuf("pu%d" % i, C, F32) for i in range(2)]

from contextlib import ExitStack

import concourse.mybir as mybir

K, J, R, T, Z, M, O, C, N, S = 512, 512, 512, 1024, 512, 1024, 256, 512, 256, 1024
FLOPS = 2 * K * R * J + 2 * Z * R * J + 2 * R * N * C

F32 = mybir.dt.float32
BF16 = mybir.dt.bfloat16
I32 = mybir.dt.int32
U32 = mybir.dt.uint32
U16 = mybir.dt.uint16
U8 = mybir.dt.uint8
FP8X4 = mybir.dt.float8_e4m3fn_x4
FP4X4 = mybir.dt.float4_e2m1fn_x4
COPY = mybir.ActivationFunctionType.Copy
ALU = mybir.AluOpType

P = 128
PACK = 4
QUADRANTS = 4
HALF = 256


def tile_picked_tokens_plain_bank_compareexchange_store_plain_kernel(
    tc, xt_words, xt_scales, w_words, w_scales, xo_words, xo_scales, w2_words, w2_scales,
    sa, sb, vs_words, vs_scales, offs, offs2, offs3, offs4, offs5, offs6, offs7, out,
):
    nc = tc.nc
    with ExitStack() as ctx:
        lists = ctx.enter_context(tc.tile_pool(name="lists", bufs=1))
        pool = ctx.enter_context(tc.tile_pool(name="pool", bufs=1))
        psum = ctx.enter_context(tc.psum_pool(name="psum", bufs=1))

        def sbuf(name, cols, dtype):
            return pool.tile([P, cols], dtype, name=name, align_bytes=64)

        def load_list(name, source):
            tile = lists.tile(list(source.shape), U16, name=name)
            nc.sync.dma_start(tile[:], source)
            return tile

        def load_e4m3_words(queue, name, source, cols):
            tile = sbuf(name, cols, U32)
            queue.dma_start(tile[:].bitcast(I32), source[0].rearrange("p n t -> p (n t)").bitcast(I32))
            return tile

        def load_e2m1_words(queue, name, source, cols):
            tile = sbuf(name, cols, U16)
            queue.dma_start(tile[:].bitcast(I32), source[0].bitcast(I32))
            return tile

        def load_scale_rows(queues, tile, source, quadrants):
            for q in quadrants:
                rows = source[0, 4 * q : 4 * q + 4, :].bitcast(I32)
                queues[q].dma_start(tile[32 * q : 32 * q + 4, :].bitcast(I32), rows)

        def zeroed_scales(engine, name, cols):
            tile = sbuf(name, cols, U8)
            engine.memset(tile[:].bitcast(I32), 0)
            return tile

        def load_scales(queues, name, source, cols, engine=nc.vector):
            tile = zeroed_scales(engine, name, cols)
            load_scale_rows(queues, tile, source, range(QUADRANTS))
            return tile

        def load_row_factors(name, source):
            tile = pool.tile([P, PACK], F32, name=name)
            nc.sync.dma_start(tile[:], source.rearrange("(p t) o -> p (t o)", t=PACK))
            return tile

        sync4 = [nc.sync] * QUADRANTS
        list2 = load_list("list2", offs2)
        xo_w = load_e2m1_words(nc.scalar, "xo_w", xo_words, M)
        xo_s = load_scales([nc.sync, nc.scalar, nc.sync, nc.scalar], "xo_s", xo_scales, M, nc.gpsimd)
        list1 = load_list("list1", offs)
        xt_w = load_e4m3_words(nc.scalar, "xt_w", xt_words, T)
        w2_s = load_scales(sync4, "w2_s", w2_scales, R)
        xt_s = zeroed_scales(nc.vector, "xt_s", T)
        load_scale_rows(sync4, xt_s, xt_scales, range(0, 2))
        w2_w = load_e4m3_words(nc.sync, "w2_w", w2_words, R)
        w_w = load_e2m1_words(nc.sync, "w_w", w_words, R)
        load_scale_rows(sync4, xt_s, xt_scales, range(2, QUADRANTS))
        w_s = load_scales(sync4, "w_s", w_scales, R)
        list3 = load_list("list3", offs3)
        sa_t = load_row_factors("sa_t", sa)
        list4 = load_list("list4", offs4)
        sb_t = load_row_factors("sb_t", sb)
        list7 = load_list("list7", offs7)
        vs_w = load_e4m3_words(nc.sync, "vs_w", vs_words, S)
        vs_s = load_scales(sync4, "vs_s", vs_scales, S)
        list5 = load_list("list5", offs5)
        list6 = load_list("list6", offs6)

        pl = [sbuf("pl%d" % i, C, F32) for i in range(2)]
        pu = [sbuf("pu%d" % i, C, F32) for i in range(2)]
        for engine, i in ((nc.vector, 0), (nc.gpsimd, 1)):
            engine.memset(pl[i][:], 0.0)
            engine.memset(pu[i][:], 0.0)

        xo_sg = sbuf("xo_sg", J, U8)
        xo_wg = sbuf("xo_wg", J, U16)
        xt_wg = sbuf("xt_wg", J, U32)
        xt_sg = sbuf("xt_sg", J, U8)
        nc.vector.tensor_copy(xo_wg[:], xo_w[:].indirect(list2[:]))
        nc.vector.tensor_copy(xo_sg[:], xo_s[:].indirect(list2[:]))
        nc.vector.tensor_copy(xt_wg[:], xt_w[:].indirect(list1[:]))

        w2_wd = sbuf("w2_wd", R, U32)
        w2_sd = sbuf("w2_sd", R, U8)
        w_wd = sbuf("w_wd", R, U16)
        w_sd = sbuf("w_sd", R, U8)
        early, late = slice(0, 2), slice(2, PACK)
        for dealt, raw in ((w2_wd, w2_w), (w_wd, w_w)):
            for tiles in (early, late):
                nc.scalar.copy(
                    dealt[:].rearrange("p (t m) -> p m t", t=PACK)[:, :, tiles],
                    raw[:].rearrange("p (m t) -> p m t", t=PACK)[:, :, tiles],
                )
        for dealt, raw, tiles in ((w2_sd, w2_s, slice(0, PACK)), (w_sd, w_s, early), (w_sd, w_s, late)):
            nc.gpsimd.tensor_copy(
                dealt[:].rearrange("p (t m) -> p t m", t=PACK)[:, tiles, :],
                raw[:].rearrange("p (m t) -> p t m", t=PACK)[:, tiles, :],
            )

        pieces = [(0, slice(0, HALF)), (0, slice(HALF, J))] + [(t, slice(0, J)) for t in range(1, PACK)]
        acc = [psum.tile([P, cols.stop - cols.start], F32, name="acc%d" % i) for i, (t, cols) in enumerate(pieces)]
        a = [sbuf("a%d" % t, J, F32) for t in range(PACK)]

        def notes_pass(i, first):
            t, cols = pieces[i]
            rows = slice(P * t, P * (t + 1))
            nc.tensor.matmul_mx(
                acc[i][:], lhsT=w2_wd[:, rows].bitcast(FP8X4), lhsT_scale=w2_sd[:, rows],
                rhs=xo_wg[:, cols].bitcast(FP4X4), rhs_scale=xo_sg[:, cols], start=first, stop=not first,
            )

        def tokens_pass(i, first):
            t, cols = pieces[i]
            rows = slice(P * t, P * (t + 1))
            nc.tensor.matmul_mx(
                acc[i][:], lhsT=w_wd[:, rows].bitcast(FP4X4), lhsT_scale=w_sd[:, rows],
                rhs=xt_wg[:, cols].bitcast(FP8X4), rhs_scale=xt_sg[:, cols], start=first, stop=not first,
            )

        notes_pass(0, True)
        notes_pass(1, True)
        notes_pass(2, True)
        for h in range(2):
            cols = pieces[h][1]
            nc.vector.tensor_copy(xt_sg[:, cols], xt_s[:].indirect(list1[:, 16 * h : 16 * (h + 1)]))
            tokens_pass(h, False)
            nc.scalar.copy(a[0][:, cols], acc[h][:])
        tokens_pass(2, False)
        nc.vector.tensor_copy(a[1][:], acc[2][:])
        for t in range(2, PACK):
            tokens_pass(t + 1, True)
            notes_pass(t + 1, False)
            nc.vector.tensor_copy(a[t][:], acc[t + 1][:])

        lo = [sbuf("lo%d" % t, O, F32) for t in range(PACK)]
        hi = [sbuf("hi%d" % t, O, F32) for t in range(PACK)]
        hid4 = [sbuf("hid4_%d" % h, PACK * HALF, BF16) for h in range(2)]

        def compare(t):
            f1 = sbuf("f1_%d" % t, O, F32)
            f2 = sbuf("f2_%d" % t, O, F32)
            nc.scalar.activation(f1[:], a[t][:].indirect(list3[:]), COPY, scale=sa_t[:, t : t + 1])
            nc.scalar.activation(f2[:], a[t][:].indirect(list4[:]), COPY, scale=sb_t[:, t : t + 1])
            nc.vector.tensor_tensor(lo[t][:], f1[:], f2[:], ALU.min)
            nc.vector.tensor_tensor(hi[t][:], f1[:], f2[:], ALU.max)

        def place(t):
            nc.scalar.activation(pl[t % 2][:].indirect(list5[:]), lo[t][:], COPY)
            nc.scalar.activation(pu[t % 2][:].indirect(list6[:]), hi[t][:], COPY)

        def add_up(t):
            hid = [sbuf("hid%d_%d" % (t, h), HALF, BF16) for h in range(2)]
            for h in range(2):
                cols = slice(HALF * h, HALF * (h + 1))
                nc.vector.tensor_tensor(hid[h][:], pl[t % 2][:, cols], pu[t % 2][:, cols], ALU.add)
            for h in range(2):
                nc.vector.tensor_copy(hid4[h][:, t : PACK * HALF : PACK], hid[h][:])

        vs_wg = sbuf("vs_wg", N, U32)
        vs_sg = sbuf("vs_sg", N, U8)
        compare(0)
        for t in range(PACK):
            if t + 1 < PACK:
                compare(t + 1)
            place(t)
            if t == 0:
                nc.vector.tensor_copy(vs_wg[:], vs_w[:].indirect(list7[:]))
                nc.vector.tensor_copy(vs_sg[:], vs_s[:].indirect(list7[:]))
            add_up(t)

        codes = [sbuf("codes%d" % h, HALF, U32) for h in range(2)]
        scales = [sbuf("scales%d" % h, HALF, U8) for h in range(2)]
        for h in range(2):
            nc.vector.quantize_mx(out=codes[h][:].bitcast(FP8X4), scales=scales[h][:], in_=hid4[h][:])
        for h in range(2):
            cols = slice(HALF * h, HALF * (h + 1))
            for b in range(2):
                rows = slice(P * b, P * (b + 1))
                y = psum.tile([P, HALF], F32, name="y%d_%d" % (h, b), tag=("y%d" % b) if h == 0 else ("acc%d" % b))
                nc.tensor.matmul_mx(
                    y[:], lhsT=vs_wg[:, rows].bitcast(FP8X4), lhsT_scale=vs_sg[:, rows],
                    rhs=codes[h][:].bitcast(FP8X4), rhs_scale=scales[h][:], start=True, stop=True,
                )
                result = sbuf("result%d_%d" % (h, b), HALF, F32)
                if h == 1 and b == 1:
                    nc.vector.tensor_copy(result[:], y[:])
                    nc.sync.dma_start(out[rows, cols], result[:])
                else:
                    nc.scalar.copy(result[:], y[:])
                    (nc.scalar if h == 1 else nc.sync).dma_start(out[rows, cols], result[:])
